import numpy as np
import ml_dtypes


def mxq(x, axis, fmt="e4m3"):
    dtype, down = {"e4m3": (ml_dtypes.float8_e4m3fn, 7), "e5m2": (ml_dtypes.float8_e5m2, 14)}[fmt]
    v = np.moveaxis(np.asarray(x, np.float32).astype(ml_dtypes.bfloat16).astype(np.float64), axis, -1)
    blocks = v.reshape(v.shape[:-1] + (-1, 32))
    amax = np.abs(blocks).max(-1, keepdims=True)
    byte = np.maximum(np.where(amax > 0, np.frexp(amax)[1] - 1 + 127, 0) - down, 1)
    scale = np.exp2(byte - 127.0)
    codes = (blocks / scale).astype(np.float32).astype(dtype).astype(np.float64)
    return np.moveaxis((codes * scale).reshape(v.shape), -1, axis)


WIDE = False


def mx_kscale(k):
    if not WIDE:
        return np.ones(k)
    levels = np.array([10, -10, 5, -5, 0])
    if k % 512:
        return np.exp2(np.random.permutation(np.resize(levels, k // 32))).repeat(32)
    a = np.empty((k // 512, 16))
    for p in range(k // 512):
        a[p, :8] = np.random.permutation(np.resize(levels, 8))
        for g in range(8):
            far = levels[np.abs(levels - a[p, g]) >= 10]
            a[p, g + 8] = far[np.random.randint(len(far))]
    return np.exp2(a.ravel()).repeat(32)


def f64(x):
    return np.asarray(x).astype(np.float64)


def striped(idx):
    return np.tile(idx.reshape(-1, 16).T, (8, 1)).astype(np.uint16)


def unstriped(offs):
    return offs[:16].T.reshape(-1).astype(np.int64)


E2M1 = np.array([0.0, 0.5, 1.0, 1.5, 2.0, 3.0, 4.0, 6.0, -0.0, -0.5, -1.0, -1.5, -2.0, -3.0, -4.0, -6.0])


def pack_weight(w, fmt):
    k, n = w.shape
    w = f64(np.asarray(w, np.float32).astype(ml_dtypes.bfloat16)).reshape(k // 32, 32, n)
    amax = np.abs(w).max(1)
    if fmt == "e4m3":
        byte = np.frexp(amax)[1] - 1 + 127 - 7
    else:
        mant, ex = np.frexp(amax / 6.0)
        byte = np.where(mant > 0.5, ex, ex - 1) + 127
    byte = np.clip(np.where(amax > 0, byte, 1), 1, 254)
    scaled = (w * np.exp2(127.0 - byte)[:, None, :]).reshape(k, n).astype(np.float32)
    by_word = np.ascontiguousarray(scaled.reshape(k // 512, 128, 4, n).transpose(0, 1, 3, 2))
    if fmt == "e4m3":
        words = by_word.astype(ml_dtypes.float8_e4m3fn).view(np.uint8)
    else:
        c = by_word.astype(ml_dtypes.float4_e2m1fn).view(np.uint8) & 0xF
        words = (c[..., 0::2] | (c[..., 1::2] << 4)).reshape(k // 512, 128, 2 * n)
    return np.ascontiguousarray(words), np.ascontiguousarray(byte.astype(np.uint8).reshape(k // 512, 16, n))


def unpack_weight(words, scales, fmt):
    g, _, n = scales.shape
    words = np.ascontiguousarray(words).reshape(g, 128, n, -1)
    if fmt == "e4m3":
        vals = words.view(ml_dtypes.float8_e4m3fn).astype(np.float64)
    else:
        nib = np.empty((g, 128, n, 4), np.uint8)
        nib[..., 0::2] = words & 0xF
        nib[..., 1::2] = words >> 4
        vals = E2M1[nib]
    vals = vals * np.repeat(np.exp2(scales.astype(np.float64) - 127.0), 8, axis=1)[..., None]
    return vals.transpose(0, 1, 3, 2).reshape(g * 512, n)


def gelu(v):
    return 0.5 * v * (1.0 + np.tanh(np.sqrt(2.0 / np.pi) * (v + 0.044715 * v**3)))


K, T, S, M, H, S2, T3, T2, P = 1024, 2048, 512, 512, 1024, 512, 2048, 1024, 512


def setup_inputs():
    n = np.random.standard_normal
    s = mx_kscale(K)[:, None]
    u1 = mx_kscale(M)[:, None]
    u = mx_kscale(H)[:, None]
    tab_words, tab_scales = pack_weight(n((K, T)) * s, "e4m3")
    w2_words, w2_scales = pack_weight(n((M, H)) * 1.4 / np.sqrt(M) / u1 * u.T, "e2m1")
    tab2_words, tab2_scales = pack_weight(n((H, T3)) / np.sqrt(H) / u, "e4m3")
    return {
        "tab_words": tab_words, "tab_scales": tab_scales,
        "offs": striped(np.random.permutation(T)[:S]),
        "w1": (n((K, M)) * 1.3 / np.sqrt(K) / s).astype(np.float32),
        "gain": (np.exp(0.3 * n(M)) * u1[:, 0]).astype(np.float32),
        "w2_words": w2_words, "w2_scales": w2_scales,
        "w3": (n((K, H)) / np.sqrt(K) / s * u.T).astype(np.float32),
        "page0": (n((H, T2)) * u).astype(np.float32),
        "wgs": np.exp(0.3 * n((128, S))).astype(np.float32),
        "offs3": striped(np.random.permutation(T2)[:S]),
        "tab2_words": tab2_words, "tab2_scales": tab2_scales,
        "offs2": striped(np.random.permutation(T3)[:S2]),
        "pos1": striped(np.random.permutation(T2)[:P]),
        "pos2": striped(np.random.permutation(T2)[:P]),
        "back": (0.8 * n((S2, P))).astype(np.float32),
    }


def reference(tab_words, tab_scales, offs, w1, gain, w2_words, w2_scales, w3, page0, wgs, offs3,
              tab2_words, tab2_scales, offs2, pos1, pos2, back):
    v = unpack_weight(tab_words, tab_scales, "e4m3")[:, unstriped(offs)]
    v2 = unpack_weight(tab2_words, tab2_scales, "e4m3")[:, unstriped(offs2)]
    d = np.tanh(mxq(f64(w1), 0, "e4m3").T @ v) * f64(gain)[:, None]
    b = unpack_weight(w2_words, w2_scales, "e2m1").T @ mxq(d, 0, "e4m3")
    h = np.maximum(b, mxq(f64(w3), 0, "e4m3").T @ v)
    page = f64(page0).copy()
    page[:, unstriped(offs3)] = np.tile(f64(wgs), (H // 128, 1)) * h
    e = v2.T @ mxq(page, 0, "e4m3")
    bg = f64(back)
    e1 = e[:, unstriped(pos1)] - bg
    e2 = e[:, unstriped(pos2)] - bg
    return e1 * e2

@@ -1,0 +1,296 @@
+from contextlib import ExitStack
+
+import concourse.mybir as mybir
+from concourse.masks import make_identity
+
+K, T, S, M, H, S2, T2, NPAIR = 1024, 2048, 512, 512, 1024, 512, 1024, 512
+FLOPS = 2 * (K * M * S + M * H * S + K * H * S + H * S2 * T2)
+
+F32 = mybir.dt.float32
+BF16 = mybir.dt.bfloat16
+I32 = mybir.dt.int32
+U32 = mybir.dt.uint32
+U16 = mybir.dt.uint16
+U8 = mybir.dt.uint8
+FP8X4 = mybir.dt.float8_e4m3fn_x4
+FP4X4 = mybir.dt.float4_e2m1fn_x4
+ALU = mybir.AluOpType
+TANH = mybir.ActivationFunctionType.Tanh
+
+P = 128
+PACK = 4
+PASS = P * PACK
+BANK = 512
+
+
+def tile_list_cluster_star_vetting_kernel(
+    tc, tab_words, tab_scales, offs, w1, gain, w2_words, w2_scales, w3, page0, wgs, offs3,
+    tab2_words, tab2_scales, offs2, pos1, pos2, back, out,
+):
+    nc = tc.nc
+    with ExitStack() as ctx:
+        held = ctx.enter_context(tc.tile_pool(name="held", bufs=1))
+        ring = ctx.enter_context(tc.tile_pool(name="ring", bufs=2))
+        psum = ctx.enter_context(tc.psum_pool(name="psum", bufs=1))
+
+        def keep(name, shape, dtype, tag=None):
+            return held.tile(shape, dtype, name=name, tag=tag or name, align_bytes=64)
+
+        def bank(index, name):
+            return psum.tile([P, BANK], F32, name=name, tag="bank%d" % index)
+
+        def load_list(name, source):
+            tile = held.tile([P, S // 16], U16, name=name)
+            nc.sync.dma_start(tile[:], source)
+            return tile
+
+        def load_words(name, words, a):
+            tile = keep(name, [P, T], U32)
+            nc.sync.dma_start(tile[:].bitcast(I32), words[a].rearrange("p t i -> p (t i)").bitcast(I32))
+            return tile
+
+        def load_scale_rows(tile, scales):
+            passes = scales.shape[0]
+            for q in range(4):
+                nc.sync.dma_start(
+                    tile[32 * q : 32 * q + 4 * passes, :].bitcast(I32),
+                    scales[:, 4 * q : 4 * q + 4, :].bitcast(I32),
+                )
+
+        def load_weight(name, w, a, b):
+            tile = keep(name, [P, PACK, PASS], F32)
+            rows = w[a * PASS : (a + 1) * PASS, b * PASS : (b + 1) * PASS]
+            nc.sync.dma_start(tile[:], rows.rearrange("(p i) c -> p i c", i=PACK))
+            return tile
+
+        def load_page(b, t):
+            tile = keep("page%d%d" % (b, t), [P, T2], F32)
+            rows = page0[b * PASS : (b + 1) * PASS, :].rearrange("(p i) c -> p i c", i=PACK)
+            nc.sync.dma_start(tile[:], rows[:, t, :])
+            return tile
+
+        def interleave_weight(copy, raw, name, tag):
+            staged = keep(name, [P, PACK, P, PACK], BF16, tag=tag)
+            copy(staged[:].rearrange("p t m i -> p m i t"), raw[:].rearrange("p i (m t) -> p m i t", t=PACK))
+            return staged
+
+        def quantize(name, source, tag=None):
+            width = source.shape[1] // PACK
+            codes = keep(name + "_codes", [P, width], U32, tag=tag)
+            scales = keep(name + "_scales", [P, width], U8)
+            nc.vector.quantize_mx(out=codes[:].bitcast(FP8X4), scales=scales[:], in_=source)
+            return codes, scales
+
+        def quantize_weight(name, staged):
+            return quantize(name, staged[:].rearrange("p t m i -> p (t m i)"))
+
+        def gather(name, dtype, window, offsets):
+            tile = keep(name, [P, S], dtype)
+            nc.vector.tensor_copy(tile[:], window[:].indirect(offsets[:]))
+            return tile
+
+        tab_sc = keep("tab_sc", [P, T], U8)
+        w2_sc = keep("w2_sc", [P, H], U8)
+        tab2_sc = keep("tab2_sc", [P, T], U8)
+        for tile in (tab_sc, w2_sc, tab2_sc):
+            nc.vector.memset(tile[:].bitcast(I32), 0)
+        identity = keep("identity", [P, P], F32)
+        make_identity(nc, identity[:])
+
+        w1_raw = [load_weight("w1_raw0", w1, 0, 0)]
+        idx = load_list("idx", offs)
+        load_scale_rows(tab_sc, tab_scales)
+        wgs_rows = keep("wgs_rows", [P, S], F32)
+        nc.sync.dma_start(wgs_rows[:], wgs)
+        w2_raw = keep("w2_raw", [P, 2 * H], U8)
+        nc.sync.dma_start(w2_raw[:].bitcast(I32), w2_words[0].bitcast(I32))
+        w1_raw.append(load_weight("w1_raw1", w1, 1, 0))
+        load_scale_rows(w2_sc, w2_scales)
+        gains = keep("gains", [P, PACK], F32)
+        nc.sync.dma_start(gains[:], gain.rearrange("(p t) -> p t", t=PACK))
+        tab_w = [load_words("tab_w%d" % a, tab_words, a) for a in range(2)]
+        w3_raw = {(a, 0): load_weight("w3_raw%d0" % a, w3, a, 0) for a in range(2)}
+        idx3 = load_list("idx3", offs3)
+        order = [(0, 0), (0, 1), (0, 2), (1, 2), (0, 3), (1, 0), (1, 1), (1, 3)]
+        page = {}
+        for a in range(2):
+            page[order[a]] = load_page(*order[a])
+            w3_raw[(a, 1)] = load_weight("w3_raw%d1" % a, w3, a, 1)
+        for key in order[2:4]:
+            page[key] = load_page(*key)
+        idx2 = load_list("idx2", offs2)
+        load_scale_rows(tab2_sc, tab2_scales)
+        tab2_w = [load_words("tab2_w%d" % a, tab2_words, a) for a in range(2)]
+        for key in order[4:]:
+            page[key] = load_page(*key)
+        p1 = load_list("p1", pos1)
+        p2 = load_list("p2", pos2)
+
+        w1_q = []
+        for a in range(2):
+            staged = interleave_weight(nc.vector.tensor_copy, w1_raw[a], "w1_bf%d" % a, "staged%d" % a)
+            w1_q.append(quantize_weight("w1_%d" % a, staged))
+        backs = keep("backs", [P, PACK, NPAIR], F32, tag="w1_raw0")
+        nc.sync.dma_start(backs[:], back.rearrange("(m p) j -> p m j", p=P))
+
+        turned = bank(4, "turned")
+        for jb in range(4):
+            nc.tensor.transpose(turned[:, jb * P : (jb + 1) * P], wgs_rows[:, jb * P : (jb + 1) * P], identity[:])
+        dealt = keep("dealt", [P, 4, PACK, 4, 32], F32, tag="w3_codes_stage")
+        for jb in range(4):
+            source = turned[:, jb * P : (jb + 1) * P].rearrange("p (q t) -> p t q", t=PACK)
+            nc.scalar.copy(dealt[:, jb], source.unsqueeze(2).to_broadcast([P, PACK, 4, 32]))
+        wg = keep("wg", [P, PACK, S], F32)
+        for t in range(PACK):
+            back_turned = bank(5 + t % 3, "back_turned%d" % t)
+            for jb in range(4):
+                nc.tensor.transpose(
+                    back_turned[:, jb * P : (jb + 1) * P],
+                    dealt[:, jb, t].rearrange("p r q -> p (r q)"),
+                    identity[:],
+                )
+            nc.scalar.copy(wg[:, t, :], back_turned[:])
+
+        w2_codes = keep("w2_codes", [P, 2, PACK, P, 2], U8)
+        w2_planes = keep("w2_planes", [P, 2, PACK, P], U8)
+        nc.vector.tensor_copy(w2_codes[:], w2_raw[:].rearrange("p (b q t e) -> p b t q e", b=2, t=PACK, e=2))
+        nc.vector.tensor_copy(w2_planes[:], w2_sc[:].rearrange("p (b q t) -> p b t q", b=2, t=PACK))
+
+        v_sc = gather("v_sc", U8, tab_sc, idx)
+        v_w = [gather("v_w0", U32, tab_w[0], idx), keep("v_w1", [P, S], U32)]
+        for half in range(2):
+            nc.vector.tensor_copy(
+                v_w[1][:, half * 256 : (half + 1) * 256], tab_w[1][:].indirect(idx[:, half * 16 : (half + 1) * 16])
+            )
+
+        d_codes = keep("d_codes", [P, S], U32)
+        d_scales = keep("d_scales", [P, S], U8)
+        d_banks = [bank(c, "d_bank%d" % c) for c in range(4)]
+        for a in range(2):
+            for c in range(4):
+                cols = slice(c * P, (c + 1) * P)
+                for t in range(PACK):
+                    chan = slice(t * P, (t + 1) * P)
+                    nc.tensor.matmul_mx(
+                        out=d_banks[c][:, chan],
+                        lhsT=w1_q[a][0][:, chan].bitcast(FP8X4), lhsT_scale=w1_q[a][1][:, chan],
+                        rhs=v_w[a][:, cols].bitcast(FP8X4), rhs_scale=v_sc[4 * a :, cols],
+                        start=(a == 0 and t == 0), stop=(a == 1 and t == PACK - 1),
+                    )
+        for c in range(4):
+            cols = slice(c * P, (c + 1) * P)
+            bent = keep("bent%d" % c, [P, P, PACK], F32, tag="staged0" if c == 2 else "bent%d" % (c % 2))
+            nc.scalar.activation(bent[:], d_banks[c][:].rearrange("p (t j) -> p j t", t=PACK), TANH)
+            d_bf = keep("d_bf%d" % c, [P, P, PACK], BF16, tag="staged1" if c == 3 else "d_bf%d" % (c % 2))
+            nc.vector.tensor_tensor(d_bf[:], bent[:], gains[:].unsqueeze(1).to_broadcast([P, P, PACK]), ALU.mult)
+            nc.vector.quantize_mx(
+                out=d_codes[:, cols].bitcast(FP8X4), scales=d_scales[:, cols],
+                in_=d_bf[:].rearrange("p j t -> p (j t)"),
+            )
+
+        w3_q = {}
+
+        def prepare_w3(b, copies):
+            for a in range(2):
+                staged = interleave_weight(copies[a], w3_raw[(a, b)], "w3_bf%d%d" % (a, b), "staged%d" % a)
+                w3_q[(a, b)] = quantize_weight("w3_%d%d" % (a, b), staged)
+
+        prepare_w3(0, (nc.scalar.copy, nc.vector.tensor_copy))
+
+        from_d = {}
+
+        def product_with_w2(n):
+            b, t = order[n]
+            acc = bank(4 + n % 2, "b_bank%d" % n)
+            nc.tensor.matmul_mx(
+                out=acc[:],
+                lhsT=w2_codes[:, b, t].rearrange("p q e -> p (q e)").bitcast(FP4X4), lhsT_scale=w2_planes[:, b, t],
+                rhs=d_codes[:].bitcast(FP8X4), rhs_scale=d_scales[:],
+                start=True, stop=True,
+            )
+            from_d[(b, t)] = keep("from_d%d" % n, [P, S], F32)
+            nc.scalar.copy(from_d[(b, t)][:], acc[:])
+
+        c_banks = [6, 7, 0, 1, 2, 3, 4, 5]
+        woven = {}
+        page_q = {}
+
+        def features(n):
+            b, t = order[n]
+            acc = bank(c_banks[n], "c_bank%d" % n)
+            chan = slice(t * P, (t + 1) * P)
+            for a in range(2):
+                nc.tensor.matmul_mx(
+                    out=acc[:],
+                    lhsT=w3_q[(a, b)][0][:, chan].bitcast(FP8X4), lhsT_scale=w3_q[(a, b)][1][:, chan],
+                    rhs=v_w[a][:].bitcast(FP8X4), rhs_scale=v_sc[4 * a :, :],
+                    start=(a == 0), stop=(a == 1),
+                )
+            h = ring.tile([P, S], F32, name="h")
+            nc.vector.tensor_tensor(h[:], acc[:], from_d[(b, t)][:], ALU.max)
+            return h
+
+        def place(n, h):
+            b, t = order[n]
+            nc.vector.tensor_tensor(page[(b, t)][:].indirect(idx3[:]), h[:], wg[:, t, :], ALU.mult)
+
+        def weave(n):
+            b, t = order[n]
+            for half in range(2):
+                if (b, half) not in woven:
+                    tag = "w3_raw%d1" % half if b == 0 else None
+                    woven[(b, half)] = keep("woven%d%d" % (b, half), [P, BANK, PACK], BF16, tag=tag)
+                last = n == len(order) - 1 and half == 0
+                copy = nc.vector.tensor_copy if last else nc.scalar.copy
+                copy(woven[(b, half)][:, :, t], page[(b, t)][:, half * BANK : (half + 1) * BANK])
+
+        def quantize_page(b):
+            for half in range(2):
+                page_q[(b, half)] = quantize(
+                    "page_q%d%d" % (b, half), woven[(b, half)][:].rearrange("p j t -> p (j t)"),
+                    tag="from_d%d" % (5 + half) if b == 0 else None,
+                )
+
+        v2_w = []
+        v2_sc = []
+        for n in range(3):
+            product_with_w2(n)
+        place(0, features(0))
+        place(1, features(1))
+        prepare_w3(1, (nc.scalar.copy, nc.scalar.copy))
+        for n in range(3, len(order)):
+            product_with_w2(n)
+        weave(0)
+        weave(1)
+        for n in range(2, len(order)):
+            place(n, features(n))
+            weave(n)
+            if n == 4:
+                v2_sc.append(gather("v2_sc", U8, tab2_sc, idx2))
+                v2_w.extend(gather("v2_w%d" % a, U32, tab2_w[a], idx2) for a in range(2))
+            if n == 6:
+                quantize_page(0)
+        quantize_page(1)
+
+        e_banks = {}
+        for b in range(2):
+            for m in range(4):
+                cand = slice(m * P, (m + 1) * P)
+                for half in range(2):
+                    if b == 0:
+                        e_banks[(m, half)] = bank(c_banks[2 * m + half], "e_bank%d%d" % (m, half))
+                    nc.tensor.matmul_mx(
+                        out=e_banks[(m, half)][:],
+                        lhsT=v2_w[b][:, cand].bitcast(FP8X4), lhsT_scale=v2_sc[0][4 * b :, cand],
+                        rhs=page_q[(b, half)][0][:].bitcast(FP8X4), rhs_scale=page_q[(b, half)][1][:],
+                        start=(b == 0), stop=(b == 1),
+                    )
+        for m in range(4):
+            scores = ring.tile([P, T2], F32, name="scores")
+            for half in range(2):
+                nc.scalar.copy(scores[:, half * BANK : (half + 1) * BANK], e_banks[(m, half)][:])
+            pair = keep("pair%d" % m, [P, 3, NPAIR], F32, tag="w3_raw%d0" % (m % 2))
+            nc.vector.tensor_tensor(pair[:, 0, :], scores[:].indirect(p1[:]), backs[:, m, :], ALU.subtract)
+            nc.vector.tensor_tensor(pair[:, 1, :], scores[:].indirect(p2[:]), backs[:, m, :], ALU.subtract)
+            nc.vector.tensor_tensor(pair[:, 2, :], pair[:, 0, :], pair[:, 1, :], ALU.mult)
+            nc.sync.dma_start(out[m * P : (m + 1) * P, :], pair[:, 2, :])

@@ -69,9 +69,10 @@ def tile_list_cluster_star_vetting_kernel(
             nc.sync.dma_start(tile[:], rows[:, t, :])
             return tile
 
-        def interleave_weight(copy, raw, name, tag):
-            staged = keep(name, [P, PACK, P, PACK], BF16, tag=tag)
-            copy(staged[:].rearrange("p t m i -> p m i t"), raw[:].rearrange("p i (m t) -> p m i t", t=PACK))
+        def interleave_weight(copy, raw, name, tag, first=0, count=PACK):
+            staged = keep(name, [P, count, P, PACK], BF16, tag=tag)
+            source = raw[:].rearrange("p i (m t) -> p m i t", t=PACK)[:, :, :, first : first + count]
+            copy(staged[:].rearrange("p t m i -> p m i t"), source)
             return staged
 
         def quantize(name, source, tag=None):
@@ -92,8 +93,9 @@ def tile_list_cluster_star_vetting_kernel(
         tab_sc = keep("tab_sc", [P, T], U8)
         w2_sc = keep("w2_sc", [P, H], U8)
         tab2_sc = keep("tab2_sc", [P, T], U8)
-        for tile in (tab_sc, w2_sc, tab2_sc):
+        for tile in (tab_sc, w2_sc):
             nc.vector.memset(tile[:].bitcast(I32), 0)
+        nc.gpsimd.memset(tab2_sc[:].bitcast(I32), 0)
         identity = keep("identity", [P, P], F32)
         make_identity(nc, identity[:])
 
@@ -102,16 +104,17 @@ def tile_list_cluster_star_vetting_kernel(
         load_scale_rows(tab_sc, tab_scales)
         wgs_rows = keep("wgs_rows", [P, S], F32)
         nc.sync.dma_start(wgs_rows[:], wgs)
-        w2_raw = keep("w2_raw", [P, 2 * H], U8)
-        nc.sync.dma_start(w2_raw[:].bitcast(I32), w2_words[0].bitcast(I32))
-        w1_raw.append(load_weight("w1_raw1", w1, 1, 0))
+        tab_w = [load_words("tab_w0", tab_words, 0)]
         load_scale_rows(w2_sc, w2_scales)
         gains = keep("gains", [P, PACK], F32)
         nc.sync.dma_start(gains[:], gain.rearrange("(p t) -> p t", t=PACK))
-        tab_w = [load_words("tab_w%d" % a, tab_words, a) for a in range(2)]
+        w1_raw.append(load_weight("w1_raw1", w1, 1, 0))
+        tab_w.append(load_words("tab_w1", tab_words, 1))
+        w2_raw = keep("w2_raw", [P, 2 * H], U8)
+        nc.sync.dma_start(w2_raw[:].bitcast(I32), w2_words[0].bitcast(I32))
         w3_raw = {(a, 0): load_weight("w3_raw%d0" % a, w3, a, 0) for a in range(2)}
         idx3 = load_list("idx3", offs3)
-        order = [(0, 0), (0, 1), (0, 2), (1, 2), (0, 3), (1, 0), (1, 1), (1, 3)]
+        order = [(b, t) for b in range(2) for t in range(PACK)]
         page = {}
         for a in range(2):
             page[order[a]] = load_page(*order[a])
@@ -126,42 +129,49 @@ def tile_list_cluster_star_vetting_kernel(
         p1 = load_list("p1", pos1)
         p2 = load_list("p2", pos2)
 
-        w1_q = []
-        for a in range(2):
-            staged = interleave_weight(nc.vector.tensor_copy, w1_raw[a], "w1_bf%d" % a, "staged%d" % a)
-            w1_q.append(quantize_weight("w1_%d" % a, staged))
-        backs = keep("backs", [P, PACK, NPAIR], F32, tag="w1_raw0")
-        nc.sync.dma_start(backs[:], back.rearrange("(m p) j -> p m j", p=P))
+        w1_q = {}
 
+        def prepare_w1(a, tags):
+            for pair, copy in enumerate((nc.vector.tensor_copy, nc.vector.tensor_copy)):
+                name = "w1_%d%d" % (a, pair)
+                staged = interleave_weight(copy, w1_raw[a], name + "_bf", tags[pair], 2 * pair, 2)
+                w1_q[(a, pair)] = quantize_weight(name, staged)
+
+        prepare_w1(0, ("staged0", "staged1"))
+        v_sc = gather("v_sc", U8, tab_sc, idx)
+        v_w = [gather("v_w0", U32, tab_w[0], idx), keep("v_w1", [P, S], U32)]
         turned = bank(4, "turned")
         for jb in range(4):
             nc.tensor.transpose(turned[:, jb * P : (jb + 1) * P], wgs_rows[:, jb * P : (jb + 1) * P], identity[:])
-        dealt = keep("dealt", [P, 4, PACK, 4, 32], F32, tag="w3_codes_stage")
-        for jb in range(4):
-            source = turned[:, jb * P : (jb + 1) * P].rearrange("p (q t) -> p t q", t=PACK)
-            nc.scalar.copy(dealt[:, jb], source.unsqueeze(2).to_broadcast([P, PACK, 4, 32]))
+        dealt = keep("dealt", [P, PACK, 4, 4, 32], F32, tag=None)
+        for t in range(PACK):
+            source = turned[:].rearrange("p (jb q t) -> p t jb q", jb=4, t=PACK)[:, t]
+            nc.scalar.copy(dealt[:, t], source.unsqueeze(2).to_broadcast([P, 4, 4, 32]))
         wg = keep("wg", [P, PACK, S], F32)
         for t in range(PACK):
             back_turned = bank(5 + t % 3, "back_turned%d" % t)
             for jb in range(4):
                 nc.tensor.transpose(
                     back_turned[:, jb * P : (jb + 1) * P],
-                    dealt[:, jb, t].rearrange("p r q -> p (r q)"),
+                    dealt[:, t, jb].rearrange("p r q -> p (r q)"),
                     identity[:],
                 )
             nc.scalar.copy(wg[:, t, :], back_turned[:])
 
-        w2_codes = keep("w2_codes", [P, 2, PACK, P, 2], U8)
-        w2_planes = keep("w2_planes", [P, 2, PACK, P], U8)
-        nc.vector.tensor_copy(w2_codes[:], w2_raw[:].rearrange("p (b q t e) -> p b t q e", b=2, t=PACK, e=2))
-        nc.vector.tensor_copy(w2_planes[:], w2_sc[:].rearrange("p (b q t) -> p b t q", b=2, t=PACK))
-
-        v_sc = gather("v_sc", U8, tab_sc, idx)
-        v_w = [gather("v_w0", U32, tab_w[0], idx), keep("v_w1", [P, S], U32)]
+        prepare_w1(1, ("tab_w0", "staged1"))
         for half in range(2):
             nc.vector.tensor_copy(
                 v_w[1][:, half * 256 : (half + 1) * 256], tab_w[1][:].indirect(idx[:, half * 16 : (half + 1) * 16])
             )
+        backs = keep("backs", [P, PACK, NPAIR], F32, tag="w1_raw0")
+        nc.sync.dma_start(backs[:], back.rearrange("(m p) j -> p m j", p=P))
+
+        w2_codes = keep("w2_codes", [P, 2, PACK, 2 * P], U8, tag="tab_w1")
+        w2_planes = keep("w2_planes", [P, 2, PACK, P], U8)
+        nc.vector.tensor_copy(
+            w2_codes[:].bitcast(U16), w2_raw[:].bitcast(U16).rearrange("p (b q t) -> p b t q", b=2, t=PACK)
+        )
+        nc.vector.tensor_copy(w2_planes[:], w2_sc[:].rearrange("p (b q t) -> p b t q", b=2, t=PACK))
 
         d_codes = keep("d_codes", [P, S], U32)
         d_scales = keep("d_scales", [P, S], U8)
@@ -170,32 +180,38 @@ def tile_list_cluster_star_vetting_kernel(
             for c in range(4):
                 cols = slice(c * P, (c + 1) * P)
                 for t in range(PACK):
-                    chan = slice(t * P, (t + 1) * P)
+                    chan = slice(t % 2 * P, (t % 2 + 1) * P)
+                    codes, scales = w1_q[(a, t // 2)]
                     nc.tensor.matmul_mx(
-                        out=d_banks[c][:, chan],
-                        lhsT=w1_q[a][0][:, chan].bitcast(FP8X4), lhsT_scale=w1_q[a][1][:, chan],
+                        out=d_banks[c][:, t * P : (t + 1) * P],
+                        lhsT=codes[:, chan].bitcast(FP8X4), lhsT_scale=scales[:, chan],
                         rhs=v_w[a][:, cols].bitcast(FP8X4), rhs_scale=v_sc[4 * a :, cols],
                         start=(a == 0 and t == 0), stop=(a == 1 and t == PACK - 1),
                     )
+        d_bf = keep("d_bf", [P, S, PACK], BF16)
         for c in range(4):
             cols = slice(c * P, (c + 1) * P)
-            bent = keep("bent%d" % c, [P, P, PACK], F32, tag="staged0" if c == 2 else "bent%d" % (c % 2))
+            bent = keep("bent%d" % c, [P, P, PACK], F32)
             nc.scalar.activation(bent[:], d_banks[c][:].rearrange("p (t j) -> p j t", t=PACK), TANH)
-            d_bf = keep("d_bf%d" % c, [P, P, PACK], BF16, tag="staged1" if c == 3 else "d_bf%d" % (c % 2))
-            nc.vector.tensor_tensor(d_bf[:], bent[:], gains[:].unsqueeze(1).to_broadcast([P, P, PACK]), ALU.mult)
-            nc.vector.quantize_mx(
-                out=d_codes[:, cols].bitcast(FP8X4), scales=d_scales[:, cols],
-                in_=d_bf[:].rearrange("p j t -> p (j t)"),
+            nc.vector.tensor_tensor(
+                d_bf[:, cols, :], bent[:], gains[:].unsqueeze(1).to_broadcast([P, P, PACK]), ALU.mult
             )
+            if c % 2 == 1:
+                done = slice((c - 1) * P, (c + 1) * P)
+                nc.vector.quantize_mx(
+                    out=d_codes[:, done].bitcast(FP8X4), scales=d_scales[:, done],
+                    in_=d_bf[:, done, :].rearrange("p j t -> p (j t)"),
+                )
 
         w3_q = {}
 
-        def prepare_w3(b, copies):
-            for a in range(2):
-                staged = interleave_weight(copies[a], w3_raw[(a, b)], "w3_bf%d%d" % (a, b), "staged%d" % a)
-                w3_q[(a, b)] = quantize_weight("w3_%d%d" % (a, b), staged)
+        def prepare_w3(a, b, pair, copy, tag):
+            name = "w3_%d%d%d" % (a, b, pair)
+            staged = interleave_weight(copy, w3_raw[(a, b)], name + "_bf", tag, 2 * pair, 2)
+            w3_q[(a, b, pair)] = quantize_weight(name, staged)
 
-        prepare_w3(0, (nc.scalar.copy, nc.vector.tensor_copy))
+        prepare_w3(0, 0, 0, nc.scalar.copy, "bent2")
+        prepare_w3(1, 0, 0, nc.vector.tensor_copy, "d_bf")
 
         from_d = {}
 
@@ -204,7 +220,7 @@ def tile_list_cluster_star_vetting_kernel(
             acc = bank(4 + n % 2, "b_bank%d" % n)
             nc.tensor.matmul_mx(
                 out=acc[:],
-                lhsT=w2_codes[:, b, t].rearrange("p q e -> p (q e)").bitcast(FP4X4), lhsT_scale=w2_planes[:, b, t],
+                lhsT=w2_codes[:, b, t].bitcast(FP4X4), lhsT_scale=w2_planes[:, b, t],
                 rhs=d_codes[:].bitcast(FP8X4), rhs_scale=d_scales[:],
                 start=True, stop=True,
             )
@@ -212,21 +228,24 @@ def tile_list_cluster_star_vetting_kernel(
             nc.scalar.copy(from_d[(b, t)][:], acc[:])
 
         c_banks = [6, 7, 0, 1, 2, 3, 4, 5]
-        woven = {}
         page_q = {}
 
         def features(n):
             b, t = order[n]
             acc = bank(c_banks[n], "c_bank%d" % n)
-            chan = slice(t * P, (t + 1) * P)
+            chan = slice(t % 2 * P, (t % 2 + 1) * P)
             for a in range(2):
+                codes, scales = w3_q[(a, b, t // 2)]
                 nc.tensor.matmul_mx(
                     out=acc[:],
-                    lhsT=w3_q[(a, b)][0][:, chan].bitcast(FP8X4), lhsT_scale=w3_q[(a, b)][1][:, chan],
+                    lhsT=codes[:, chan].bitcast(FP8X4), lhsT_scale=scales[:, chan],
                     rhs=v_w[a][:].bitcast(FP8X4), rhs_scale=v_sc[4 * a :, :],
                     start=(a == 0), stop=(a == 1),
                 )
-            h = ring.tile([P, S], F32, name="h")
+            if n == len(order) - 1:
+                h = keep("h_last", [P, S], F32)
+            else:
+                h = ring.tile([P, S], F32, name="h")
             nc.vector.tensor_tensor(h[:], acc[:], from_d[(b, t)][:], ALU.max)
             return h
 
@@ -234,57 +253,87 @@ def tile_list_cluster_star_vetting_kernel(
             b, t = order[n]
             nc.vector.tensor_tensor(page[(b, t)][:].indirect(idx3[:]), h[:], wg[:, t, :], ALU.mult)
 
+        planar = keep("planar", [P, PACK, T2], BF16, tag="dealt")
+        woven = [keep("woven1%d" % half, [P, BANK, PACK], BF16) for half in range(2)]
+
         def weave(n):
             b, t = order[n]
-            for half in range(2):
-                if (b, half) not in woven:
-                    tag = "w3_raw%d1" % half if b == 0 else None
-                    woven[(b, half)] = keep("woven%d%d" % (b, half), [P, BANK, PACK], BF16, tag=tag)
-                last = n == len(order) - 1 and half == 0
-                copy = nc.vector.tensor_copy if last else nc.scalar.copy
-                copy(woven[(b, half)][:, :, t], page[(b, t)][:, half * BANK : (half + 1) * BANK])
+            if b == 0:
+                nc.scalar.copy(planar[:, t, :], page[(b, t)][:])
+            else:
+                for half in range(2):
+                    nc.scalar.copy(woven[half][:, :, t], page[(b, t)][:, half * BANK : (half + 1) * BANK])
 
-        def quantize_page(b):
-            for half in range(2):
-                page_q[(b, half)] = quantize(
-                    "page_q%d%d" % (b, half), woven[(b, half)][:].rearrange("p j t -> p (j t)"),
-                    tag="from_d%d" % (5 + half) if b == 0 else None,
-                )
+        v2 = {}
 
-        v2_w = []
-        v2_sc = []
-        for n in range(3):
-            product_with_w2(n)
+        def gather_candidates(part, tags):
+            entries = idx2[:, part * 16 : (part + 1) * 16]
+            scales = keep("v2_sc%d" % part, [P, 256], U8, tag=tags[0])
+            words = keep("v2_w%d" % part, [P, 2, 256], U32, tag=tags[1])
+            nc.vector.tensor_copy(scales[:], tab2_sc[:].indirect(entries))
+            for a in range(2):
+                nc.vector.tensor_copy(words[:, a, :], tab2_w[a][:].indirect(entries))
+            v2[part] = (words, scales)
+
+        product_with_w2(0)
+        product_with_w2(1)
+        prepare_w3(0, 0, 1, nc.scalar.copy, "bent3")
+        prepare_w3(1, 0, 1, nc.scalar.copy, "bent2")
+        product_with_w2(2)
         place(0, features(0))
         place(1, features(1))
-        prepare_w3(1, (nc.scalar.copy, nc.scalar.copy))
-        for n in range(3, len(order)):
+        prepare_w3(0, 1, 0, nc.scalar.copy, "staged0")
+        prepare_w3(1, 1, 0, nc.scalar.copy, "staged1")
+        product_with_w2(3)
+        prepare_w3(0, 1, 1, nc.scalar.copy, "bent0")
+        prepare_w3(1, 1, 1, nc.scalar.copy, "bent1")
+        for n in range(4, len(order)):
             product_with_w2(n)
         weave(0)
         weave(1)
         for n in range(2, len(order)):
             place(n, features(n))
             weave(n)
+            if n == PACK - 1:
+                woven0 = keep("woven0", [P, T2, PACK], BF16, tag="w3_raw11")
+                for half in range(2):
+                    cols = slice(half * BANK, (half + 1) * BANK)
+                    nc.scalar.copy(
+                        woven0[:, cols, :].rearrange("p (c i) t -> p c t i", i=4),
+                        planar[:, :, cols].rearrange("p t (c i) -> p c t i", i=4),
+                    )
             if n == 4:
-                v2_sc.append(gather("v2_sc", U8, tab2_sc, idx2))
-                v2_w.extend(gather("v2_w%d" % a, U32, tab2_w[a], idx2) for a in range(2))
-            if n == 6:
-                quantize_page(0)
-        quantize_page(1)
+                gather_candidates(0, (None, None))
+        codes, scales = quantize("page_q0", woven0[:].rearrange("p j t -> p (j t)"), tag="h_last")
+        for half in range(2):
+            cols = slice(half * BANK, (half + 1) * BANK)
+            page_q[(0, half)] = (codes[:, cols], scales[:, cols])
 
         e_banks = {}
-        for b in range(2):
-            for m in range(4):
-                cand = slice(m * P, (m + 1) * P)
-                for half in range(2):
-                    if b == 0:
-                        e_banks[(m, half)] = bank(c_banks[2 * m + half], "e_bank%d%d" % (m, half))
-                    nc.tensor.matmul_mx(
-                        out=e_banks[(m, half)][:],
-                        lhsT=v2_w[b][:, cand].bitcast(FP8X4), lhsT_scale=v2_sc[0][4 * b :, cand],
-                        rhs=page_q[(b, half)][0][:].bitcast(FP8X4), rhs_scale=page_q[(b, half)][1][:],
-                        start=(b == 0), stop=(b == 1),
-                    )
+
+        def score(m, b):
+            words, scales = v2[m // 2]
+            cand = slice(m % 2 * P, (m % 2 + 1) * P)
+            for half in range(2):
+                if b == 0:
+                    e_banks[(m, half)] = bank(c_banks[2 * m + half], "e_bank%d%d" % (m, half))
+                nc.tensor.matmul_mx(
+                    out=e_banks[(m, half)][:],
+                    lhsT=words[:, b, cand].bitcast(FP8X4), lhsT_scale=scales[4 * b :, cand],
+                    rhs=page_q[(b, half)][0][:].bitcast(FP8X4), rhs_scale=page_q[(b, half)][1][:],
+                    start=(b == 0), stop=(b == 1),
+                )
+
+        score(0, 0)
+        score(1, 0)
+        for half in range(2):
+            page_q[(1, half)] = quantize("page_q1%d" % half, woven[half][:].rearrange("p j t -> p (j t)"))
+        score(0, 1)
+        score(1, 1)
+        gather_candidates(1, ("woven10", "woven11"))
+        for m in range(2, 4):
+            score(m, 0)
+            score(m, 1)
         for m in range(4):
             scores = ring.tile([P, T2], F32, name="scores")
             for half in range(2):
@@ -292,5 +341,8 @@ def tile_list_cluster_star_vetting_kernel(
             pair = keep("pair%d" % m, [P, 3, NPAIR], F32, tag="w3_raw%d0" % (m % 2))
             nc.vector.tensor_tensor(pair[:, 0, :], scores[:].indirect(p1[:]), backs[:, m, :], ALU.subtract)
             nc.vector.tensor_tensor(pair[:, 1, :], scores[:].indirect(p2[:]), backs[:, m, :], ALU.subtract)
-            nc.vector.tensor_tensor(pair[:, 2, :], pair[:, 0, :], pair[:, 1, :], ALU.mult)
-            nc.sync.dma_start(out[m * P : (m + 1) * P, :], pair[:, 2, :])
+            pieces = 2 if m == 3 else 1
+            for piece in range(pieces):
+                cols = slice(piece * NPAIR // pieces, (piece + 1) * NPAIR // pieces)
+                nc.vector.tensor_tensor(pair[:, 2, cols], pair[:, 0, cols], pair[:, 1, cols], ALU.mult)
+                nc.sync.dma_start(out[m * P : (m + 1) * P, cols], pair[:, 2, cols])

@@ -104,12 +104,11 @@ def tile_list_cluster_star_vetting_kernel(
         load_scale_rows(tab_sc, tab_scales)
         wgs_rows = keep("wgs_rows", [P, S], F32)
         nc.sync.dma_start(wgs_rows[:], wgs)
-        tab_w = [load_words("tab_w0", tab_words, 0)]
+        w1_raw.append(load_weight("w1_raw1", w1, 1, 0))
         load_scale_rows(w2_sc, w2_scales)
         gains = keep("gains", [P, PACK], F32)
         nc.sync.dma_start(gains[:], gain.rearrange("(p t) -> p t", t=PACK))
-        w1_raw.append(load_weight("w1_raw1", w1, 1, 0))
-        tab_w.append(load_words("tab_w1", tab_words, 1))
+        tab_w = [load_words("tab_w%d" % a, tab_words, a) for a in range(2)]
         w2_raw = keep("w2_raw", [P, 2 * H], U8)
         nc.sync.dma_start(w2_raw[:].bitcast(I32), w2_words[0].bitcast(I32))
         w3_raw = {(a, 0): load_weight("w3_raw%d0" % a, w3, a, 0) for a in range(2)}
@@ -139,7 +138,6 @@ def tile_list_cluster_star_vetting_kernel(
 
         prepare_w1(0, ("staged0", "staged1"))
         v_sc = gather("v_sc", U8, tab_sc, idx)
-        v_w = [gather("v_w0", U32, tab_w[0], idx), keep("v_w1", [P, S], U32)]
         turned = bank(4, "turned")
         for jb in range(4):
             nc.tensor.transpose(turned[:, jb * P : (jb + 1) * P], wgs_rows[:, jb * P : (jb + 1) * P], identity[:])
@@ -158,11 +156,13 @@ def tile_list_cluster_star_vetting_kernel(
                 )
             nc.scalar.copy(wg[:, t, :], back_turned[:])
 
-        prepare_w1(1, ("tab_w0", "staged1"))
-        for half in range(2):
-            nc.vector.tensor_copy(
-                v_w[1][:, half * 256 : (half + 1) * 256], tab_w[1][:].indirect(idx[:, half * 16 : (half + 1) * 16])
-            )
+        prepare_w1(1, ("staged0", "staged1"))
+        v_w = [keep("v_w%d" % a, [P, S], U32) for a in range(2)]
+        for a in range(2):
+            for half in range(2):
+                nc.vector.tensor_copy(
+                    v_w[a][:, half * 256 : (half + 1) * 256], tab_w[a][:].indirect(idx[:, half * 16 : (half + 1) * 16])
+                )
         backs = keep("backs", [P, PACK, NPAIR], F32, tag="w1_raw0")
         nc.sync.dma_start(backs[:], back.rearrange("(m p) j -> p m j", p=P))
 

from contextlib import ExitStack

import concourse.mybir as mybir
from concourse.masks import make_identity

K, T, S, M, H, S2, T2, NPAIR = 1024, 2048, 512, 512, 1024, 512, 1024, 512
FLOPS = 2 * (K * M * S + M * H * S + K * H * S + H * S2 * T2)

F32 = mybir.dt.float32
BF16 = mybir.dt.bfloat16
I32 = mybir.dt.int32
U32 = mybir.dt.uint32
U16 = mybir.dt.uint16
U8 = mybir.dt.uint8
FP8X4 = mybir.dt.float8_e4m3fn_x4
FP4X4 = mybir.dt.float4_e2m1fn_x4
ALU = mybir.AluOpType
TANH = mybir.ActivationFunctionType.Tanh

P = 128
PACK = 4
PASS = P * PACK
BANK = 512


def tile_list_cluster_star_vetting_kernel(
    tc, tab_words, tab_scales, offs, w1, gain, w2_words, w2_scales, w3, page0, wgs, offs3,
    tab2_words, tab2_scales, offs2, pos1, pos2, back, out,
):
    nc = tc.nc
    with ExitStack() as ctx:
        held = ctx.enter_context(tc.tile_pool(name="held", bufs=1))
        ring = ctx.enter_context(tc.tile_pool(name="ring", bufs=2))
        psum = ctx.enter_context(tc.psum_pool(name="psum", bufs=1))

        def keep(name, shape, dtype, tag=None):
            return held.tile(shape, dtype, name=name, tag=tag or name, align_bytes=64)

        def bank(index, name):
            return psum.tile([P, BANK], F32, name=name, tag="bank%d" % index)

        def load_list(name, source):
            tile = held.tile([P, S // 16], U16, name=name)
            nc.sync.dma_start(tile[:], source)
            return tile

        def load_words(name, words, a):
            tile = keep(name, [P, T], U32)
            nc.sync.dma_start(tile[:].bitcast(I32), words[a].rearrange("p t i -> p (t i)").bitcast(I32))
            return tile

        def load_scale_rows(tile, scales):
            passes = scales.shape[0]
            for q in range(4):
                nc.sync.dma_start(
                    tile[32 * q : 32 * q + 4 * passes, :].bitcast(I32),
                    scales[:, 4 * q : 4 * q + 4, :].bitcast(I32),
                )

        def load_weight(name, w, a, b):
            tile = keep(name, [P, PACK, PASS], F32)
            rows = w[a * PASS : (a + 1) * PASS, b * PASS : (b + 1) * PASS]
            nc.sync.dma_start(tile[:], rows.rearrange("(p i) c -> p i c", i=PACK))
            return tile

        def load_page(b, t):
            tile = keep("page%d%d" % (b, t), [P, T2], F32)
            rows = page0[b * PASS : (b + 1) * PASS, :].rearrange("(p i) c -> p i c", i=PACK)
            nc.sync.dma_start(tile[:], rows[:, t, :])
            return tile

        def interleave_weight(copy, raw, name, tag, first=0, count=PACK):
            staged = keep(name, [P, count, P, PACK], BF16, tag=tag)
            source = raw[:].rearrange("p i (m t) -> p m i t", t=PACK)[:, :, :, first : first + count]
            copy(staged[:].rearrange("p t m i -> p m i t"), source)
            return staged

        def quantize(name, source, tag=None):
            width = source.shape[1] // PACK
            codes = keep(name + "_codes", [P, width], U32, tag=tag)
            scales = keep(name + "_scales", [P, width], U8)
            nc.vector.quantize_mx(out=codes[:].bitcast(FP8X4), scales=scales[:], in_=source)
            return codes, scales

        def quantize_weight(name, staged):
            return quantize(name, staged[:].rearrange("p t m i -> p (t m i)"))

        def gather(name, dtype, window, offsets):
            tile = keep(name, [P, S], dtype)
            nc.vector.tensor_copy(tile[:], window[:].indirect(offsets[:]))
            return tile

        tab_sc = keep("tab_sc", [P, T], U8)
        w2_sc = keep("w2_sc", [P, H], U8)
        tab2_sc = keep("tab2_sc", [P, T], U8)
        for tile in (tab_sc, w2_sc):
            nc.vector.memset(tile[:].bitcast(I32), 0)
        nc.gpsimd.memset(tab2_sc[:].bitcast(I32), 0)
        identity = keep("identity", [P, P], F32)
        make_identity(nc, identity[:])

        w1_raw = [load_weight("w1_raw0", w1, 0, 0)]
        idx = load_list("idx", offs)
        load_scale_rows(tab_sc, tab_scales)
        wgs_rows = keep("wgs_rows", [P, S], F32)
        nc.sync.dma_start(wgs_rows[:], wgs)
        w1_raw.append(load_weight("w1_raw1", w1, 1, 0))
        load_scale_rows(w2_sc, w2_scales)
        gains = keep("gains", [P, PACK], F32)
        nc.sync.dma_start(gains[:], gain.rearrange("(p t) -> p t", t=PACK))
        tab_w = [load_words("tab_w%d" % a, tab_words, a) for a in range(2)]
        w2_raw = keep("w2_raw", [P, 2 * H], U8)
        nc.sync.dma_start(w2_raw[:].bitcast(I32), w2_words[0].bitcast(I32))
        w3_raw = {(a, 0): load_weight("w3_raw%d0" % a, w3, a, 0) for a in range(2)}
        idx3 = load_list("idx3", offs3)
        order = [(b, t) for b in range(2) for t in range(PACK)]
        page = {}
        for a in range(2):
            page[order[a]] = load_page(*order[a])
            w3_raw[(a, 1)] = load_weight("w3_raw%d1" % a, w3, a, 1)
        for key in order[2:4]:
            page[key] = load_page(*key)
        idx2 = load_list("idx2", offs2)
        load_scale_rows(tab2_sc, tab2_scales)
        tab2_w = [load_words("tab2_w%d" % a, tab2_words, a) for a in range(2)]
        for key in order[4:]:
            page[key] = load_page(*key)
        p1 = load_list("p1", pos1)
        p2 = load_list("p2", pos2)

        w1_q = {}

        def prepare_w1(a, tags):
            for pair, copy in enumerate((nc.vector.tensor_copy, nc.vector.tensor_copy)):
                name = "w1_%d%d" % (a, pair)
                staged = interleave_weight(copy, w1_raw[a], name + "_bf", tags[pair], 2 * pair, 2)
                w1_q[(a, pair)] = quantize_weight(name, staged)

        prepare_w1(0, ("staged0", "staged1"))
        v_sc = gather("v_sc", U8, tab_sc, idx)
        turned = bank(4, "turned")
        for jb in range(4):
            nc.tensor.transpose(turned[:, jb * P : (jb + 1) * P], wgs_rows[:, jb * P : (jb + 1) * P], identity[:])
        dealt = keep("dealt", [P, PACK, 4, 4, 32], F32, tag=None)
        for t in range(PACK):
            source = turned[:].rearrange("p (jb q t) -> p t jb q", jb=4, t=PACK)[:, t]
            nc.scalar.copy(dealt[:, t], source.unsqueeze(2).to_broadcast([P, 4, 4, 32]))
        wg = keep("wg", [P, PACK, S], F32)
        for t in range(PACK):
            back_turned = bank(5 + t % 3, "back_turned%d" % t)
            for jb in range(4):
                nc.tensor.transpose(
                    back_turned[:, jb * P : (jb + 1) * P],
                    dealt[:, t, jb].rearrange("p r q -> p (r q)"),
                    identity[:],
                )
            nc.scalar.copy(wg[:, t, :], back_turned[:])

        prepare_w1(1, ("staged0", "staged1"))
        v_w = [keep("v_w%d" % a, [P, S], U32) for a in range(2)]
        for a in range(2):
            for half in range(2):
                nc.vector.tensor_copy(
                    v_w[a][:, half * 256 : (half + 1) * 256], tab_w[a][:].indirect(idx[:, half * 16 : (half + 1) * 16])
                )
        backs = keep("backs", [P, PACK, NPAIR], F32, tag="w1_raw0")
        nc.sync.dma_start(backs[:], back.rearrange("(m p) j -> p m j", p=P))

        w2_codes = keep("w2_codes", [P, 2, PACK, 2 * P], U8, tag="tab_w1")
        w2_planes = keep("w2_planes", [P, 2, PACK, P], U8)
        nc.vector.tensor_copy(
            w2_codes[:].bitcast(U16), w2_raw[:].bitcast(U16).rearrange("p (b q t) -> p b t q", b=2, t=PACK)
        )
        nc.vector.tensor_copy(w2_planes[:], w2_sc[:].rearrange("p (b q t) -> p b t q", b=2, t=PACK))

        d_codes = keep("d_codes", [P, S], U32)
        d_scales = keep("d_scales", [P, S], U8)
        d_banks = [bank(c, "d_bank%d" % c) for c in range(4)]
        for a in range(2):
            for c in range(4):
                cols = slice(c * P, (c + 1) * P)
                for t in range(PACK):
                    chan = slice(t % 2 * P, (t % 2 + 1) * P)
                    codes, scales = w1_q[(a, t // 2)]
                    nc.tensor.matmul_mx(
                        out=d_banks[c][:, t * P : (t + 1) * P],
                        lhsT=codes[:, chan].bitcast(FP8X4), lhsT_scale=scales[:, chan],
                        rhs=v_w[a][:, cols].bitcast(FP8X4), rhs_scale=v_sc[4 * a :, cols],
                        start=(a == 0 and t == 0), stop=(a == 1 and t == PACK - 1),
                    )
        d_bf = keep("d_bf", [P, S, PACK], BF16)
        for c in range(4):
            cols = slice(c * P, (c + 1) * P)
            bent = keep("bent%d" % c, [P, P, PACK], F32)
            nc.scalar.activation(bent[:], d_banks[c][:].rearrange("p (t j) -> p j t", t=PACK), TANH)
            nc.vector.tensor_tensor(
                d_bf[:, cols, :], bent[:], gains[:].unsqueeze(1).to_broadcast([P, P, PACK]), ALU.mult
            )
            if c % 2 == 1:
                done = slice((c - 1) * P, (c + 1) * P)
                nc.vector.quantize_mx(
                    out=d_codes[:, done].bitcast(FP8X4), scales=d_scales[:, done],
                    in_=d_bf[:, done, :].rearrange("p j t -> p (j t)"),
                )

        w3_q = {}

        def prepare_w3(a, b, pair, copy, tag):
            name = "w3_%d%d%d" % (a, b, pair)
            staged = interleave_weight(copy, w3_raw[(a, b)], name + "_bf", tag, 2 * pair, 2)
            w3_q[(a, b, pair)] = quantize_weight(name, staged)

        prepare_w3(0, 0, 0, nc.scalar.copy, "bent2")
        prepare_w3(1, 0, 0, nc.vector.tensor_copy, "d_bf")

        from_d = {}

        def product_with_w2(n):
            b, t = order[n]
            acc = bank(4 + n % 2, "b_bank%d" % n)
            nc.tensor.matmul_mx(
                out=acc[:],
                lhsT=w2_codes[:, b, t].bitcast(FP4X4), lhsT_scale=w2_planes[:, b, t],
                rhs=d_codes[:].bitcast(FP8X4), rhs_scale=d_scales[:],
                start=True, stop=True,
            )
            from_d[(b, t)] = keep("from_d%d" % n, [P, S], F32)
            nc.scalar.copy(from_d[(b, t)][:], acc[:])

        c_banks = [6, 7, 0, 1, 2, 3, 4, 5]
        page_q = {}

        def features(n):
            b, t = order[n]
            acc = bank(c_banks[n], "c_bank%d" % n)
            chan = slice(t % 2 * P, (t % 2 + 1) * P)
            for a in range(2):
                codes, scales = w3_q[(a, b, t // 2)]
                nc.tensor.matmul_mx(
                    out=acc[:],
                    lhsT=codes[:, chan].bitcast(FP8X4), lhsT_scale=scales[:, chan],
                    rhs=v_w[a][:].bitcast(FP8X4), rhs_scale=v_sc[4 * a :, :],
                    start=(a == 0), stop=(a == 1),
                )
            if n == len(order) - 1:
                h = keep("h_last", [P, S], F32)
            else:
                h = ring.tile([P, S], F32, name="h")
            nc.vector.tensor_tensor(h[:], acc[:], from_d[(b, t)][:], ALU.max)
            return h

        def place(n, h):
            b, t = order[n]
            nc.vector.tensor_tensor(page[(b, t)][:].indirect(idx3[:]), h[:], wg[:, t, :], ALU.mult)

        planar = keep("planar", [P, PACK, T2], BF16, tag="dealt")
        woven = [keep("woven1%d" % half, [P, BANK, PACK], BF16) for half in range(2)]

        def weave(n):
            b, t = order[n]
            if b == 0:
                nc.scalar.copy(planar[:, t, :], page[(b, t)][:])
            else:
                for half in range(2):
                    nc.scalar.copy(woven[half][:, :, t], page[(b, t)][:, half * BANK : (half + 1) * BANK])

        v2 = {}

        def gather_candidates(part, tags):
            entries = idx2[:, part * 16 : (part + 1) * 16]
            scales = keep("v2_sc%d" % part, [P, 256], U8, tag=tags[0])
            words = keep("v2_w%d" % part, [P, 2, 256], U32, tag=tags[1])
            nc.vector.tensor_copy(scales[:], tab2_sc[:].indirect(entries))
            for a in range(2):
                nc.vector.tensor_copy(words[:, a, :], tab2_w[a][:].indirect(entries))
            v2[part] = (words, scales)

        product_with_w2(0)
        product_with_w2(1)
        prepare_w3(0, 0, 1, nc.scalar.copy, "bent3")
        prepare_w3(1, 0, 1, nc.scalar.copy, "bent2")
        product_with_w2(2)
        place(0, features(0))
        place(1, features(1))
        prepare_w3(0, 1, 0, nc.scalar.copy, "staged0")
        prepare_w3(1, 1, 0, nc.scalar.copy, "staged1")
        product_with_w2(3)
        prepare_w3(0, 1, 1, nc.scalar.copy, "bent0")
        prepare_w3(1, 1, 1, nc.scalar.copy, "bent1")
        for n in range(4, len(order)):
            product_with_w2(n)
        weave(0)
        weave(1)
        for n in range(2, len(order)):
            place(n, features(n))
            weave(n)
            if n == PACK - 1:
                woven0 = keep("woven0", [P, T2, PACK], BF16, tag="w3_raw11")
                for half in range(2):
                    cols = slice(half * BANK, (half + 1) * BANK)
                    nc.scalar.copy(
                        woven0[:, cols, :].rearrange("p (c i) t -> p c t i", i=4),
                        planar[:, :, cols].rearrange("p t (c i) -> p c t i", i=4),
                    )
            if n == 4:
                gather_candidates(0, (None, None))
        codes, scales = quantize("page_q0", woven0[:].rearrange("p j t -> p (j t)"), tag="h_last")
        for half in range(2):
            cols = slice(half * BANK, (half + 1) * BANK)
            page_q[(0, half)] = (codes[:, cols], scales[:, cols])

        e_banks = {}

        def score(m, b):
            words, scales = v2[m // 2]
            cand = slice(m % 2 * P, (m % 2 + 1) * P)
            for half in range(2):
                if b == 0:
                    e_banks[(m, half)] = bank(c_banks[2 * m + half], "e_bank%d%d" % (m, half))
                nc.tensor.matmul_mx(
                    out=e_banks[(m, half)][:],
                    lhsT=words[:, b, cand].bitcast(FP8X4), lhsT_scale=scales[4 * b :, cand],
                    rhs=page_q[(b, half)][0][:].bitcast(FP8X4), rhs_scale=page_q[(b, half)][1][:],
                    start=(b == 0), stop=(b == 1),
                )

        score(0, 0)
        score(1, 0)
        for half in range(2):
            page_q[(1, half)] = quantize("page_q1%d" % half, woven[half][:].rearrange("p j t -> p (j t)"))
        score(0, 1)
        score(1, 1)
        gather_candidates(1, ("woven10", "woven11"))
        for m in range(2, 4):
            score(m, 0)
            score(m, 1)
        for m in range(4):
            scores = ring.tile([P, T2], F32, name="scores")
            for half in range(2):
                nc.scalar.copy(scores[:, half * BANK : (half + 1) * BANK], e_banks[(m, half)][:])
            pair = keep("pair%d" % m, [P, 3, NPAIR], F32, tag="w3_raw%d0" % (m % 2))
            nc.vector.tensor_tensor(pair[:, 0, :], scores[:].indirect(p1[:]), backs[:, m, :], ALU.subtract)
            nc.vector.tensor_tensor(pair[:, 1, :], scores[:].indirect(p2[:]), backs[:, m, :], ALU.subtract)
            pieces = 2 if m == 3 else 1
            for piece in range(pieces):
                cols = slice(piece * NPAIR // pieces, (piece + 1) * NPAIR // pieces)
                nc.vector.tensor_tensor(pair[:, 2, cols], pair[:, 0, cols], pair[:, 1, cols], ALU.mult)
                nc.sync.dma_start(out[m * P : (m + 1) * P, cols], pair[:, 2, cols])
